import numpy as np
import ml_dtypes


def mxq(x, axis, fmt="e4m3"):
    dtype, down = {"e4m3": (ml_dtypes.float8_e4m3fn, 7), "e5m2": (ml_dtypes.float8_e5m2, 14)}[fmt]
    v = np.moveaxis(np.asarray(x, np.float32).astype(ml_dtypes.bfloat16).astype(np.float64), axis, -1)
    blocks = v.reshape(v.shape[:-1] + (-1, 32))
    amax = np.abs(blocks).max(-1, keepdims=True)
    byte = np.maximum(np.where(amax > 0, np.frexp(amax)[1] - 1 + 127, 0) - down, 1)
    scale = np.exp2(byte - 127.0)
    codes = (blocks / scale).astype(np.float32).astype(dtype).astype(np.float64)
    return np.moveaxis((codes * scale).reshape(v.shape), -1, axis)


WIDE = False


def mx_kscale(k):
    if not WIDE:
        return np.ones(k)
    levels = np.array([10, -10, 5, -5, 0])
    if k % 512:
        return np.exp2(np.random.permutation(np.resize(levels, k // 32))).repeat(32)
    a = np.empty((k // 512, 16))
    for p in range(k // 512):
        a[p, :8] = np.random.permutation(np.resize(levels, 8))
        for g in range(8):
            far = levels[np.abs(levels - a[p, g]) >= 10]
            a[p, g + 8] = far[np.random.randint(len(far))]
    return np.exp2(a.ravel()).repeat(32)


def f64(x):
    return np.asarray(x).astype(np.float64)


def striped(idx):
    return np.tile(idx.reshape(-1, 16).T, (8, 1)).astype(np.uint16)


def unstriped(offs):
    return offs[:16].T.reshape(-1).astype(np.int64)


E2M1 = np.array([0.0, 0.5, 1.0, 1.5, 2.0, 3.0, 4.0, 6.0, -0.0, -0.5, -1.0, -1.5, -2.0, -3.0, -4.0, -6.0])


def pack_fp4(w):
    k, n = w.shape
    w = f64(np.asarray(w, np.float32).astype(ml_dtypes.bfloat16)).reshape(k // 32, 32, n)
    amax = np.abs(w).max(1)
    mant, ex = np.frexp(amax / 6.0)
    byte = np.clip(np.where(amax > 0, np.where(mant > 0.5, ex, ex - 1) + 127, 1), 1, 254)
    scaled = (w * np.exp2(127.0 - byte)[:, None, :]).reshape(k, n).astype(np.float32)
    c = np.ascontiguousarray(scaled.reshape(k // 512, 128, 4, n).transpose(0, 1, 3, 2)).astype(ml_dtypes.float4_e2m1fn).view(np.uint8) & 0xF
    words = (c[..., 0::2] | (c[..., 1::2] << 4)).reshape(k // 512, 128, 2 * n)
    return np.ascontiguousarray(words), np.ascontiguousarray(byte.astype(np.uint8).reshape(k // 512, 16, n))


def unpack_fp4(words, scales):
    g, _, n = scales.shape
    words = np.ascontiguousarray(words).reshape(g, 128, n, 2)
    nib = np.empty((g, 128, n, 4), np.uint8)
    nib[..., 0::2] = words & 0xF
    nib[..., 1::2] = words >> 4
    vals = E2M1[nib] * np.repeat(np.exp2(scales.astype(np.float64) - 127.0), 8, axis=1)[..., None]
    return vals.transpose(0, 1, 3, 2).reshape(g * 512, n)


def relu(v):
    return np.maximum(v, 0.0)


def gelu(v):
    return 0.5 * v * (1.0 + np.tanh(np.sqrt(2.0 / np.pi) * (v + 0.044715 * v**3)))


K, T, S, D, V, H, N, U = 1024, 2048, 1024, 2, 512, 512, 256, 256
P = 2 ** 7


def setup_inputs():
    n = np.random.standard_normal
    s = mx_kscale(K)[:, None]
    u = mx_kscale(H)
    packed_w2 = pack_fp4(n((H, N)) / np.sqrt(H) / u[:, None])
    return {
        "xT": (n((K, T)) * s).astype(np.float32),
        "w1": (n((K, H)) / np.sqrt(K) / s * u).astype(np.float32),
        "w2_words": packed_w2[0],
        "w2_scales": packed_w2[1],
        "gate": (np.tile(np.random.uniform(0.2, 1.0, (D, 1, V)) / np.sqrt(D), (1, P, 1))).astype(np.float32),
        "gate2": (np.tile(np.random.uniform(0.2, 1.0, (D, 1, U)) / np.sqrt(D), (1, P, 1))).astype(np.float32),
        "offs": striped(np.random.permutation(T)[:S]),
        "pos1": striped(np.random.permutation(S)[:V]),
        "pos2": striped(np.random.permutation(S)[:V]),
        "nxt1": striped(np.random.permutation(V)[:U]),
        "nxt2": striped(np.random.permutation(V)[:U]),
    }


def reference(xT, w1, w2_words, w2_scales, gate, gate2, offs, pos1, pos2, nxt1, nxt2):
    xq = mxq(f64(xT)[:, unstriped(offs)], 0, "e4m3")
    h = gelu(mxq(f64(w1), 0, "e4m3").T @ xq)
    z = h[:, unstriped(pos1)] * f64(gate)[0, :1] + h[:, unstriped(pos2)] * f64(gate)[1, :1]
    g = relu(unpack_fp4(w2_words, w2_scales).T @ mxq(z, 0, "e4m3"))
    return g[:, unstriped(nxt1)] * f64(gate2)[0, :1] + g[:, unstriped(nxt2)] * f64(gate2)[1, :1]

@@ -1,0 +1,321 @@
+from contextlib import ExitStack
+
+import concourse.mybir as mybir
+from concourse.masks import make_identity
+
+K, T, S, V, H, N, U = 1024, 2048, 1024, 512, 512, 256, 256
+FLOPS = 2 * K * H * S + 2 * H * N * V
+
+F32 = mybir.dt.float32
+BF16 = mybir.dt.bfloat16
+I32 = mybir.dt.int32
+U32 = mybir.dt.uint32
+U16 = mybir.dt.uint16
+U8 = mybir.dt.uint8
+FP8X4 = mybir.dt.float8_e4m3fn_x4
+FP4X4 = mybir.dt.float4_e2m1fn_x4
+ACT = mybir.ActivationFunctionType
+ALU = mybir.AluOpType
+
+P = 128
+PACK = 4
+K_PASS = P * PACK
+PASSES = K // K_PASS
+BANK = 512
+
+X_CHUNKS = [[512, 512, 512, 512], [512, 512, 512, 256, 256]]
+VEC_COLS = {512: 192, 256: 160}
+W_COLS = 256
+S_PIECES = [(0, 512), (512, 256), (768, 256)]
+Z_PIECES = [(0, 256), (256, 128), (384, 128)]
+
+
+def interleave(copy, grouped, raw, c0, c1):
+    copy(
+        out=grouped[:, c0:c1, :].rearrange("p (c i) t -> p c t i", i=4),
+        in_=raw[:, :, c0:c1].rearrange("p t (c i) -> p c t i", i=4),
+    )
+
+
+def tile_picked_hop2_gelu_e_kernel(
+    tc, xT, w1, w2_words, w2_scales, gate, gate2, offs, pos1, pos2, nxt1, nxt2, out
+):
+    nc = tc.nc
+    with ExitStack() as ctx:
+        keep = ctx.enter_context(tc.tile_pool(name="keep", bufs=1))
+        psum = ctx.enter_context(tc.psum_pool(name="psum", bufs=8))
+
+        def bank(name):
+            return psum.tile([P, BANK], F32, name=name, tag="bank")
+
+        warm = keep.tile([P, 8], F32, name="warm")
+        warm_out = keep.tile([P, 8], F32, name="warm_out")
+        nc.vector.memset(warm[:], 0.0)
+        nc.scalar.activation(warm_out[:], warm[:], ACT.Gelu_apprx_tanh)
+
+        x_bytes = keep.tile([P, T], U8, name="x_bytes", align_bytes=64)
+        nc.gpsimd.memset(x_bytes[:], 0)
+        w2_bytes = keep.tile([P, N], U8, name="w2_bytes", align_bytes=64)
+        nc.gpsimd.memset(w2_bytes[:], 0)
+        ident = keep.tile([P, P], F32, name="ident")
+        make_identity(nc, ident[:])
+
+        offs_sb = keep.tile([P, S // 16], U16, name="offs_sb")
+        pos_sb = [keep.tile([P, V // 16], U16, name="pos%d" % d) for d in range(2)]
+        nxt_sb = [keep.tile([P, U // 16], U16, name="nxt%d" % d) for d in range(2)]
+
+        x_raw = {}
+        for g in range(PASSES):
+            rows = xT[g * K_PASS : (g + 1) * K_PASS, :].rearrange("(p j) w -> p j w", j=PACK)
+            c0 = 0
+            for n, width in enumerate(X_CHUNKS[g]):
+                raw = keep.tile([P, PACK, width], F32, name="x_raw%d_%d" % (g, n))
+                nc.sync.dma_start(out=raw[:], in_=rows[:, :, c0 : c0 + width])
+                x_raw[g, n] = raw
+                c0 = c0 + width
+                if g == 0 and n == 1:
+                    nc.sync.dma_start(offs_sb[:], offs)
+                    nc.sync.dma_start(pos_sb[0][:], pos1)
+                    nc.sync.dma_start(pos_sb[1][:], pos2)
+        w_raw = {}
+        for b in range(H // W_COLS):
+            for g in range(PASSES):
+                rows = w1[g * K_PASS : (g + 1) * K_PASS, :].rearrange("(p j) w -> p j w", j=PACK)
+                raw = keep.tile([P, PACK, W_COLS], F32, name="w_raw%d_%d" % (b, g))
+                nc.sync.dma_start(out=raw[:], in_=rows[:, :, b * W_COLS : (b + 1) * W_COLS])
+                w_raw[b, g] = raw
+        gate_sb = keep.tile([P, 2, V], F32, name="gate_sb")
+        nc.sync.dma_start(out=gate_sb[:], in_=gate.rearrange("d p v -> p d v"))
+        gate2_sb = keep.tile([P, 2, U], F32, name="gate2_sb")
+        nc.sync.dma_start(out=gate2_sb[:], in_=gate2.rearrange("d p v -> p d v"))
+        nc.sync.dma_start(nxt_sb[0][:], nxt1)
+        nc.sync.dma_start(nxt_sb[1][:], nxt2)
+        w2_codes = keep.tile([P, 2 * N], U8, name="w2_codes", align_bytes=64)
+        nc.sync.dma_start(out=w2_codes[:].bitcast(I32), in_=w2_words[0].bitcast(I32))
+        for q in range(4):
+            nc.sync.dma_start(
+                out=w2_bytes[32 * q : 32 * q + 4, :].bitcast(I32), in_=w2_scales[0, 4 * q : 4 * q + 4, :].bitcast(I32)
+            )
+
+        x_words = [keep.tile([P, T], U32, name="x_words%d" % g, align_bytes=64) for g in range(PASSES)]
+        picked_words = {}
+
+        def pick_words(g, half, tag, cuts):
+            t = keep.tile([P, BANK], U32, name="picked%d_%d" % (g, half), tag=tag, align_bytes=64)
+            for o0, sw in cuts:
+                s0 = half * BANK + o0
+                nc.vector.tensor_copy(
+                    t[:, o0 : o0 + sw], x_words[g][:].indirect(offs_sb[:, s0 // 16 : (s0 + sw) // 16])
+                )
+            picked_words[g, half] = t
+
+        for g in range(PASSES):
+            c0 = 0
+            for n, width in enumerate(X_CHUNKS[g]):
+                grouped = keep.tile([P, width, PACK], BF16, name="x_bf%d_%d" % (g, n), align_bytes=64)
+                split = VEC_COLS[width]
+                interleave(nc.vector.tensor_copy, grouped, x_raw[g, n], 0, split)
+                interleave(nc.scalar.copy, grouped, x_raw[g, n], split, width)
+                nc.vector.quantize_mx(
+                    out=x_words[g][:, c0 : c0 + width].bitcast(FP8X4),
+                    scales=x_bytes[4 * g : P, c0 : c0 + width],
+                    in_=grouped[:].rearrange("p w j -> p (w j)"),
+                )
+                c0 = c0 + width
+            if g == 0:
+                pick_words(0, 0, "picked0", [(0, BANK)])
+                pick_words(0, 1, "picked1", [(0, BANK)])
+        picked_bytes = keep.tile([P, S], U8, name="picked_bytes", align_bytes=64)
+        nc.vector.tensor_copy(picked_bytes[:], x_bytes[:].indirect(offs_sb[:]))
+
+        w_words = {}
+        w_bytes = {}
+        for c in range(PACK):
+            for g in range(PASSES):
+                w_words[c, g] = keep.tile([P, P], U32, name="w_words%d_%d" % (c, g), align_bytes=64)
+                w_bytes[c, g] = keep.tile([P, P], U8, name="w_bytes%d_%d" % (c, g), align_bytes=64)
+
+        def quantise_w(b, g, tag):
+            stage = keep.tile([P, PACK, W_COLS // PACK, PACK], BF16, name="w_bf%d_%d" % (b, g), tag=tag, align_bytes=64)
+            nc.scalar.copy(
+                out=stage[:].rearrange("p t m j -> p m j t"),
+                in_=w_raw[b, g][:].rearrange("p j (m t) -> p m j t", t=PACK),
+            )
+            flat = stage[:].rearrange("p t m j -> p (t m j)")
+            nc.vector.quantize_mx(out=w_words[b, g][:].bitcast(FP8X4), scales=w_bytes[b, g][:], in_=flat[:, 0 : 2 * W_COLS])
+            cols = slice(64 * b, 64 * (b + 1))
+            for t in (2, 3):
+                nc.vector.quantize_mx(
+                    out=w_words[t, g][:, cols].bitcast(FP8X4),
+                    scales=w_bytes[t, g][:, cols],
+                    in_=flat[:, t * W_COLS : (t + 1) * W_COLS],
+                )
+
+        h = [keep.tile([P, S], F32, name="h%d" % c) for c in range(PACK)]
+
+        def first(c, cuts):
+            for s0, sw in cuts:
+                acc = bank("acc")
+                half, o0 = divmod(s0, BANK)
+                for g in range(PASSES):
+                    nc.tensor.matmul_mx(
+                        out=acc[:, 0:sw],
+                        lhsT=w_words[c, g][:].bitcast(FP8X4),
+                        lhsT_scale=w_bytes[c, g][:],
+                        rhs=picked_words[g, half][:, o0 : o0 + sw].bitcast(FP8X4),
+                        rhs_scale=picked_bytes[4 * g : P, s0 : s0 + sw],
+                        start=(g == 0),
+                        stop=(g == PASSES - 1),
+                    )
+                nc.scalar.activation(h[c][:, s0 : s0 + sw], acc[:, 0:sw], ACT.Gelu_apprx_tanh)
+
+        quantise_w(0, 0, "w_stage00")
+        quantise_w(0, 1, "w_stage01")
+        pick_words(1, 0, "w_stage00", [(0, BANK)])
+        pick_words(1, 1, "w_stage01", [(0, 256), (256, 256)])
+        quantise_w(1, 0, "w_stage10")
+        quantise_w(1, 1, "w_stage11")
+        first(0, S_PIECES)
+        for c in (1, 2, 3):
+            first(c, [(0, BANK), (BANK, BANK)])
+
+        g_sb = [keep.tile([P, V], F32, name="g%d" % m) for m in range(N // P)]
+        z_bf = [keep.tile([P, w, PACK], BF16, name="z_bf%d" % n, align_bytes=64) for n, (v0, w) in enumerate(Z_PIECES)]
+        z_q = {}
+
+        def fetch_terms(c, v0, w, terms, e):
+            for d in range(2):
+                nc.vector.tensor_tensor(
+                    terms[d][:, e, :],
+                    h[c][:].indirect(pos_sb[d][:, v0 // 16 : (v0 + w) // 16]),
+                    gate_sb[:, d, v0 : v0 + w],
+                    ALU.mult,
+                )
+
+        def new_terms(name, rows, w):
+            return [keep.tile([P, rows, w], F32, name="%s_%d" % (name, d)) for d in range(2)]
+
+        def turn_and_add(dst, terms, e, blk):
+            for d in range(2):
+                nc.tensor.matmul(
+                    dst, terms[d][:, e, blk * P : (blk + 1) * P], ident[:], start=(d == 0), stop=(d == 1), is_transpose=True
+                )
+
+        low = keep.tile([P, V // P, 2, 64, 2], BF16, name="low")
+        for b in range(2):
+            terms = new_terms("low_terms%d" % b, 1, V)
+            fetch_terms(b, 0, V, terms, 0)
+            summed = bank("summed")
+            for blk in range(V // P):
+                turn_and_add(summed[:, blk * P : (blk + 1) * P], terms, 0, blk)
+            nc.scalar.copy(out=low[:, :, b, :, :], in_=summed[:].rearrange("p (k e m) -> p k m e", e=2, m=64))
+        low_words = low[:].rearrange("p k b m e -> p (k b m e)").bitcast(F32)
+        back = [bank("back%d" % n) for n in range(len(Z_PIECES))]
+        for n, (v0, w) in enumerate(Z_PIECES):
+            for blk in range(w // P):
+                k = v0 // P + blk
+                nc.tensor.transpose(back[n][:, blk * P : (blk + 1) * P], low_words[:, k * P : (k + 1) * P], ident[:])
+        last = len(Z_PIECES) - 1
+        v_last, w_last = Z_PIECES[last]
+        nc.scalar.copy(
+            out=z_bf[last][:].rearrange("p v t -> p (v t)").bitcast(F32).rearrange("p (v u) -> p v u", u=2)[:, :, 0],
+            in_=back[last][:, 0:w_last],
+        )
+
+        high = {}
+
+        def sum_high(n, between=None):
+            v0, w = Z_PIECES[n]
+            terms = new_terms("high_terms%d" % n, 2, w)
+            summed = bank("summed")
+            for e in range(2):
+                fetch_terms(2 + e, v0, w, terms, e)
+                for blk in range(w // P):
+                    turn_and_add(summed[:, (e * (w // P) + blk) * P : (e * (w // P) + blk + 1) * P], terms, e, blk)
+                if e == 0 and between is not None:
+                    turn_back(between)
+            high[n] = keep.tile([P, w // P, P, 2], BF16, name="high%d" % n)
+            nc.scalar.copy(out=high[n][:], in_=summed[:, 0 : 2 * w].rearrange("p (e k m) -> p k m e", e=2, m=P))
+
+        def turn_back(n):
+            v0, w = Z_PIECES[n]
+            words = high[n][:].rearrange("p k m e -> p (k m e)").bitcast(F32)
+            for blk in range(w // P):
+                nc.tensor.transpose(
+                    back[n][:, w + blk * P : w + (blk + 1) * P], words[:, blk * P : (blk + 1) * P], ident[:]
+                )
+            nc.scalar.copy(
+                out=z_bf[n][:].rearrange("p v t -> p (v t)").bitcast(F32).rearrange("p (v u) -> p v u", u=2),
+                in_=back[n][:, 0 : 2 * w].rearrange("p (u v) -> p v u", u=2),
+            )
+
+        def quantise_z(n):
+            v0, w = Z_PIECES[n]
+            z_words = keep.tile([P, w], U32, name="z_words%d" % n, align_bytes=64)
+            z_bytes = keep.tile([P, w], U8, name="z_bytes%d" % n, align_bytes=64)
+            nc.vector.quantize_mx(
+                out=z_words[:].bitcast(FP8X4), scales=z_bytes[:], in_=z_bf[n][:].rearrange("p v t -> p (v t)")
+            )
+            z_q[n] = (z_words, z_bytes)
+
+        def second(n, m):
+            v0, w = Z_PIECES[n]
+            acc2 = bank("acc2")
+            nc.tensor.matmul_mx(
+                out=acc2[:, 0:w],
+                lhsT=w2_codes[:, 2 * P * m : 2 * P * (m + 1)].bitcast(FP4X4),
+                lhsT_scale=w2_bytes[:, P * m : P * (m + 1)],
+                rhs=z_q[n][0][:].bitcast(FP8X4),
+                rhs_scale=z_q[n][1][:],
+                start=True,
+                stop=True,
+            )
+            nc.scalar.activation(g_sb[m][:, v0 : v0 + w], acc2[:, 0:w], ACT.Relu)
+
+        sum_high(0)
+        sum_high(1, between=0)
+        turn_back(1)
+        terms = new_terms("high_terms_last", 2, w_last)
+        for e in range(2):
+            fetch_terms(2 + e, v_last, w_last, terms, e)
+        quantise_z(0)
+        nc.vector.tensor_tensor(
+            z_bf[last][:, :, 2:4],
+            terms[0][:].rearrange("p e v -> p v e"),
+            terms[1][:].rearrange("p e v -> p v e"),
+            ALU.add,
+        )
+        quantise_z(1)
+        quantise_z(2)
+        for m in range(N // P):
+            for n in range(len(Z_PIECES)):
+                second(n, m)
+
+        roots = {}
+
+        def fetch(m, d, r0, w):
+            if (m, d) not in roots:
+                roots[m, d] = keep.tile([P, U], F32, name="root%d_%d" % (m, d))
+            nc.vector.tensor_tensor(
+                roots[m, d][:, r0 : r0 + w],
+                g_sb[m][:].indirect(nxt_sb[d][:, r0 // 16 : (r0 + w) // 16]),
+                gate2_sb[:, d, r0 : r0 + w],
+                ALU.mult,
+            )
+
+        res = [keep.tile([P, U], F32, name="res%d" % m) for m in range(N // P)]
+
+        def add(m, r0, w):
+            cols = slice(r0, r0 + w)
+            nc.vector.tensor_tensor(res[m][:, cols], roots[m, 0][:, cols], roots[m, 1][:, cols], ALU.add)
+
+        fetch(0, 0, 0, U)
+        fetch(0, 1, 0, U)
+        fetch(1, 0, 0, U)
+        add(0, 0, U)
+        nc.sync.dma_start(out=out[0:P, :], in_=res[0][:])
+        fetch(1, 1, 0, U // 2)
+        fetch(1, 1, U // 2, U // 2)
+        add(1, 0, U // 2)
+        add(1, U // 2, U // 2)
+        nc.sync.dma_start(out=out[P : 2 * P, :], in_=res[1][:])

@@ -23,8 +23,9 @@ K_PASS = P * PACK
 PASSES = K // K_PASS
 BANK = 512
 
-X_CHUNKS = [[512, 512, 512, 512], [512, 512, 512, 256, 256]]
-VEC_COLS = {512: 192, 256: 160}
+X_CHUNKS = [[1280, 768], [1024, 512, 256, 256]]
+VEC_COLS = [[640, 384], [512, 192, 96, 128]]
+Q_COLS = 512
 W_COLS = 256
 S_PIECES = [(0, 512), (512, 256), (768, 256)]
 Z_PIECES = [(0, 256), (256, 128), (384, 128)]
@@ -73,7 +74,7 @@ def tile_picked_hop2_gelu_e_kernel(
                 nc.sync.dma_start(out=raw[:], in_=rows[:, :, c0 : c0 + width])
                 x_raw[g, n] = raw
                 c0 = c0 + width
-                if g == 0 and n == 1:
+                if g == 0 and n == 0:
                     nc.sync.dma_start(offs_sb[:], offs)
                     nc.sync.dma_start(pos_sb[0][:], pos1)
                     nc.sync.dma_start(pos_sb[1][:], pos2)
@@ -85,7 +86,8 @@ def tile_picked_hop2_gelu_e_kernel(
                 nc.sync.dma_start(out=raw[:], in_=rows[:, :, b * W_COLS : (b + 1) * W_COLS])
                 w_raw[b, g] = raw
         gate_sb = keep.tile([P, 2, V], F32, name="gate_sb")
-        nc.sync.dma_start(out=gate_sb[:], in_=gate.rearrange("d p v -> p d v"))
+        for d in range(2):
+            nc.sync.dma_start(out=gate_sb[:, d, :], in_=gate[d])
         gate2_sb = keep.tile([P, 2, U], F32, name="gate2_sb")
         nc.sync.dma_start(out=gate2_sb[:], in_=gate2.rearrange("d p v -> p d v"))
         nc.sync.dma_start(nxt_sb[0][:], nxt1)
@@ -113,14 +115,16 @@ def tile_picked_hop2_gelu_e_kernel(
             c0 = 0
             for n, width in enumerate(X_CHUNKS[g]):
                 grouped = keep.tile([P, width, PACK], BF16, name="x_bf%d_%d" % (g, n), align_bytes=64)
-                split = VEC_COLS[width]
+                split = VEC_COLS[g][n]
                 interleave(nc.vector.tensor_copy, grouped, x_raw[g, n], 0, split)
                 interleave(nc.scalar.copy, grouped, x_raw[g, n], split, width)
-                nc.vector.quantize_mx(
-                    out=x_words[g][:, c0 : c0 + width].bitcast(FP8X4),
-                    scales=x_bytes[4 * g : P, c0 : c0 + width],
-                    in_=grouped[:].rearrange("p w j -> p (w j)"),
-                )
+                for q1 in range(width % Q_COLS or Q_COLS, width + 1, Q_COLS):
+                    q0 = max(0, q1 - Q_COLS)
+                    nc.vector.quantize_mx(
+                        out=x_words[g][:, c0 + q0 : c0 + q1].bitcast(FP8X4),
+                        scales=x_bytes[4 * g : P, c0 + q0 : c0 + q1],
+                        in_=grouped[:, q0:q1, :].rearrange("p w j -> p (w j)"),
+                    )
                 c0 = c0 + width
             if g == 0:
                 pick_words(0, 0, "picked0", [(0, BANK)])
@@ -135,9 +139,9 @@ def tile_picked_hop2_gelu_e_kernel(
                 w_words[c, g] = keep.tile([P, P], U32, name="w_words%d_%d" % (c, g), align_bytes=64)
                 w_bytes[c, g] = keep.tile([P, P], U8, name="w_bytes%d_%d" % (c, g), align_bytes=64)
 
-        def quantise_w(b, g, tag):
+        def quantise_w(b, g, tag, copy):
             stage = keep.tile([P, PACK, W_COLS // PACK, PACK], BF16, name="w_bf%d_%d" % (b, g), tag=tag, align_bytes=64)
-            nc.scalar.copy(
+            copy(
                 out=stage[:].rearrange("p t m j -> p m j t"),
                 in_=w_raw[b, g][:].rearrange("p j (m t) -> p m j t", t=PACK),
             )
@@ -169,12 +173,12 @@ def tile_picked_hop2_gelu_e_kernel(
                     )
                 nc.scalar.activation(h[c][:, s0 : s0 + sw], acc[:, 0:sw], ACT.Gelu_apprx_tanh)
 
-        quantise_w(0, 0, "w_stage00")
-        quantise_w(0, 1, "w_stage01")
+        quantise_w(0, 0, "w_stage00", nc.scalar.copy)
+        quantise_w(0, 1, "w_stage01", nc.scalar.copy)
         pick_words(1, 0, "w_stage00", [(0, BANK)])
         pick_words(1, 1, "w_stage01", [(0, 256), (256, 256)])
-        quantise_w(1, 0, "w_stage10")
-        quantise_w(1, 1, "w_stage11")
+        quantise_w(1, 0, "w_stage10", nc.scalar.copy)
+        quantise_w(1, 1, "w_stage11", nc.vector.tensor_copy)
         first(0, S_PIECES)
         for c in (1, 2, 3):
             first(c, [(0, BANK), (BANK, BANK)])
@@ -278,17 +282,16 @@ def tile_picked_hop2_gelu_e_kernel(
         terms = new_terms("high_terms_last", 2, w_last)
         for e in range(2):
             fetch_terms(2 + e, v_last, w_last, terms, e)
-        quantise_z(0)
         nc.vector.tensor_tensor(
             z_bf[last][:, :, 2:4],
             terms[0][:].rearrange("p e v -> p v e"),
             terms[1][:].rearrange("p e v -> p v e"),
             ALU.add,
         )
-        quantise_z(1)
-        quantise_z(2)
+        for n in (0, 2, 1):
+            quantise_z(n)
         for m in range(N // P):
-            for n in range(len(Z_PIECES)):
+            for n in (0, 2, 1):
                 second(n, m)
 
         roots = {}

@@ -22,13 +22,23 @@ PACK = 4
 K_PASS = P * PACK
 PASSES = K // K_PASS
 BANK = 512
+BANKS = 8
+PER_COLUMN = 16
+SCALE_ROWS = 4
+HOPS = 2
 
-X_CHUNKS = [[1280, 768], [1024, 512, 256, 256]]
-VEC_COLS = [[640, 384], [512, 192, 96, 128]]
-Q_COLS = 512
-W_COLS = 256
-S_PIECES = [(0, 512), (512, 256), (768, 256)]
+X_LOADS = [[1280, 768], [1024, 512, 256, 256]]
+X_ON_VECTOR = [[640, 384], [512, 192, 96, 128]]
+X_QUANT = 512
+W_HALF = H // 2
+GROUPS = W_HALF // PACK
+S_STEPS = [(0, 512), (512, 256), (768, 256)]
 Z_PIECES = [(0, 256), (256, 128), (384, 128)]
+LAST = len(Z_PIECES) - 1
+
+
+def entries(offsets, first, count):
+    return offsets[:, first // PER_COLUMN : (first + count) // PER_COLUMN]
 
 
 def interleave(copy, grouped, raw, c0, c1):
@@ -38,21 +48,25 @@ def interleave(copy, grouped, raw, c0, c1):
     )
 
 
+def as_pairs(tile):
+    return tile[:].rearrange("p v t -> p (v t)").bitcast(F32).rearrange("p (v u) -> p v u", u=2)
+
+
 def tile_picked_hop2_gelu_e_kernel(
     tc, xT, w1, w2_words, w2_scales, gate, gate2, offs, pos1, pos2, nxt1, nxt2, out
 ):
     nc = tc.nc
     with ExitStack() as ctx:
         keep = ctx.enter_context(tc.tile_pool(name="keep", bufs=1))
-        psum = ctx.enter_context(tc.psum_pool(name="psum", bufs=8))
+        psum = ctx.enter_context(tc.psum_pool(name="psum", bufs=1))
 
-        def bank(name):
-            return psum.tile([P, BANK], F32, name=name, tag="bank")
+        def bank(name, number):
+            return psum.tile([P, BANK], F32, name=name, tag="bank%d" % (number % BANKS))
 
-        warm = keep.tile([P, 8], F32, name="warm")
+        warm_in = keep.tile([P, 8], F32, name="warm_in")
         warm_out = keep.tile([P, 8], F32, name="warm_out")
-        nc.vector.memset(warm[:], 0.0)
-        nc.scalar.activation(warm_out[:], warm[:], ACT.Gelu_apprx_tanh)
+        nc.vector.memset(warm_in[:], 0.0)
+        nc.scalar.activation(warm_out[:], warm_in[:], ACT.Gelu_apprx_tanh)
 
         x_bytes = keep.tile([P, T], U8, name="x_bytes", align_bytes=64)
         nc.gpsimd.memset(x_bytes[:], 0)
@@ -61,264 +75,267 @@ def tile_picked_hop2_gelu_e_kernel(
         ident = keep.tile([P, P], F32, name="ident")
         make_identity(nc, ident[:])
 
-        offs_sb = keep.tile([P, S // 16], U16, name="offs_sb")
-        pos_sb = [keep.tile([P, V // 16], U16, name="pos%d" % d) for d in range(2)]
-        nxt_sb = [keep.tile([P, U // 16], U16, name="nxt%d" % d) for d in range(2)]
-
+        offs_sb = keep.tile([P, S // PER_COLUMN], U16, name="offs_sb")
+        pos_sb = [keep.tile([P, V // PER_COLUMN], U16, name="pos%d" % d) for d in range(HOPS)]
+        nxt_sb = [keep.tile([P, U // PER_COLUMN], U16, name="nxt%d" % d) for d in range(HOPS)]
         x_raw = {}
-        for g in range(PASSES):
-            rows = xT[g * K_PASS : (g + 1) * K_PASS, :].rearrange("(p j) w -> p j w", j=PACK)
+        for n in range(PASSES):
+            rows = xT[n * K_PASS : (n + 1) * K_PASS, :].rearrange("(p j) w -> p j w", j=PACK)
             c0 = 0
-            for n, width in enumerate(X_CHUNKS[g]):
-                raw = keep.tile([P, PACK, width], F32, name="x_raw%d_%d" % (g, n))
-                nc.sync.dma_start(out=raw[:], in_=rows[:, :, c0 : c0 + width])
-                x_raw[g, n] = raw
+            for load, width in enumerate(X_LOADS[n]):
+                x_raw[n, load] = keep.tile([P, PACK, width], F32, name="x_raw%d_%d" % (n, load))
+                nc.sync.dma_start(out=x_raw[n, load][:], in_=rows[:, :, c0 : c0 + width])
                 c0 = c0 + width
-                if g == 0 and n == 0:
+                if (n, load) == (0, 0):
                     nc.sync.dma_start(offs_sb[:], offs)
                     nc.sync.dma_start(pos_sb[0][:], pos1)
                     nc.sync.dma_start(pos_sb[1][:], pos2)
         w_raw = {}
-        for b in range(H // W_COLS):
-            for g in range(PASSES):
-                rows = w1[g * K_PASS : (g + 1) * K_PASS, :].rearrange("(p j) w -> p j w", j=PACK)
-                raw = keep.tile([P, PACK, W_COLS], F32, name="w_raw%d_%d" % (b, g))
-                nc.sync.dma_start(out=raw[:], in_=rows[:, :, b * W_COLS : (b + 1) * W_COLS])
-                w_raw[b, g] = raw
-        gate_sb = keep.tile([P, 2, V], F32, name="gate_sb")
-        for d in range(2):
+        for b in range(H // W_HALF):
+            for n in range(PASSES):
+                rows = w1[n * K_PASS : (n + 1) * K_PASS, :].rearrange("(p j) w -> p j w", j=PACK)
+                w_raw[b, n] = keep.tile([P, PACK, W_HALF], F32, name="w_raw%d_%d" % (b, n))
+                nc.sync.dma_start(out=w_raw[b, n][:], in_=rows[:, :, b * W_HALF : (b + 1) * W_HALF])
+        gate_sb = keep.tile([P, HOPS, V], F32, name="gate_sb")
+        for d in range(HOPS):
             nc.sync.dma_start(out=gate_sb[:, d, :], in_=gate[d])
-        gate2_sb = keep.tile([P, 2, U], F32, name="gate2_sb")
+        gate2_sb = keep.tile([P, HOPS, U], F32, name="gate2_sb")
         nc.sync.dma_start(out=gate2_sb[:], in_=gate2.rearrange("d p v -> p d v"))
         nc.sync.dma_start(nxt_sb[0][:], nxt1)
         nc.sync.dma_start(nxt_sb[1][:], nxt2)
         w2_codes = keep.tile([P, 2 * N], U8, name="w2_codes", align_bytes=64)
         nc.sync.dma_start(out=w2_codes[:].bitcast(I32), in_=w2_words[0].bitcast(I32))
-        for q in range(4):
+        for q in range(P // 32):
             nc.sync.dma_start(
-                out=w2_bytes[32 * q : 32 * q + 4, :].bitcast(I32), in_=w2_scales[0, 4 * q : 4 * q + 4, :].bitcast(I32)
+                out=w2_bytes[32 * q : 32 * q + SCALE_ROWS, :].bitcast(I32),
+                in_=w2_scales[0, SCALE_ROWS * q : SCALE_ROWS * (q + 1), :].bitcast(I32),
             )
 
-        x_words = [keep.tile([P, T], U32, name="x_words%d" % g, align_bytes=64) for g in range(PASSES)]
+        x_words = [keep.tile([P, T], U32, name="x_words%d" % n, align_bytes=64) for n in range(PASSES)]
         picked_words = {}
 
-        def pick_words(g, half, tag, cuts):
-            t = keep.tile([P, BANK], U32, name="picked%d_%d" % (g, half), tag=tag, align_bytes=64)
-            for o0, sw in cuts:
-                s0 = half * BANK + o0
-                nc.vector.tensor_copy(
-                    t[:, o0 : o0 + sw], x_words[g][:].indirect(offs_sb[:, s0 // 16 : (s0 + sw) // 16])
-                )
-            picked_words[g, half] = t
+        def pick_words(n, half, tag, steps):
+            picked = keep.tile([P, BANK], U32, name="picked%d_%d" % (n, half), tag=tag, align_bytes=64)
+            for s0, count in steps:
+                o0 = s0 - half * BANK
+                nc.vector.tensor_copy(picked[:, o0 : o0 + count], x_words[n][:].indirect(entries(offs_sb, s0, count)))
+            picked_words[n, half] = picked
 
-        for g in range(PASSES):
+        for n in range(PASSES):
             c0 = 0
-            for n, width in enumerate(X_CHUNKS[g]):
-                grouped = keep.tile([P, width, PACK], BF16, name="x_bf%d_%d" % (g, n), align_bytes=64)
-                split = VEC_COLS[g][n]
-                interleave(nc.vector.tensor_copy, grouped, x_raw[g, n], 0, split)
-                interleave(nc.scalar.copy, grouped, x_raw[g, n], split, width)
-                for q1 in range(width % Q_COLS or Q_COLS, width + 1, Q_COLS):
-                    q0 = max(0, q1 - Q_COLS)
+            for load, width in enumerate(X_LOADS[n]):
+                grouped = keep.tile([P, width, PACK], BF16, name="x_bf%d_%d" % (n, load), align_bytes=64)
+                split = X_ON_VECTOR[n][load]
+                interleave(nc.vector.tensor_copy, grouped, x_raw[n, load], 0, split)
+                interleave(nc.scalar.copy, grouped, x_raw[n, load], split, width)
+                for q1 in range(width % X_QUANT or X_QUANT, width + 1, X_QUANT):
+                    q0 = max(0, q1 - X_QUANT)
                     nc.vector.quantize_mx(
-                        out=x_words[g][:, c0 + q0 : c0 + q1].bitcast(FP8X4),
-                        scales=x_bytes[4 * g : P, c0 + q0 : c0 + q1],
+                        out=x_words[n][:, c0 + q0 : c0 + q1].bitcast(FP8X4),
+                        scales=x_bytes[SCALE_ROWS * n : P, c0 + q0 : c0 + q1],
                         in_=grouped[:, q0:q1, :].rearrange("p w j -> p (w j)"),
                     )
                 c0 = c0 + width
-            if g == 0:
-                pick_words(0, 0, "picked0", [(0, BANK)])
-                pick_words(0, 1, "picked1", [(0, BANK)])
+            if n == 0:
+                for half in range(S // BANK):
+                    pick_words(0, half, "picked_first%d" % half, [(half * BANK, BANK)])
         picked_bytes = keep.tile([P, S], U8, name="picked_bytes", align_bytes=64)
         nc.vector.tensor_copy(picked_bytes[:], x_bytes[:].indirect(offs_sb[:]))
 
         w_words = {}
         w_bytes = {}
         for c in range(PACK):
-            for g in range(PASSES):
-                w_words[c, g] = keep.tile([P, P], U32, name="w_words%d_%d" % (c, g), align_bytes=64)
-                w_bytes[c, g] = keep.tile([P, P], U8, name="w_bytes%d_%d" % (c, g), align_bytes=64)
+            for n in range(PASSES):
+                w_words[c, n] = keep.tile([P, P], U32, name="w_words%d_%d" % (c, n), align_bytes=64)
+                w_bytes[c, n] = keep.tile([P, P], U8, name="w_bytes%d_%d" % (c, n), align_bytes=64)
 
-        def quantise_w(b, g, tag, copy):
-            stage = keep.tile([P, PACK, W_COLS // PACK, PACK], BF16, name="w_bf%d_%d" % (b, g), tag=tag, align_bytes=64)
+        def quantise_w(b, n, copy):
+            stage = keep.tile(
+                [P, PACK, GROUPS, PACK], BF16, name="w_bf%d_%d" % (b, n), tag="w_stage%d_%d" % (b, n), align_bytes=64
+            )
             copy(
                 out=stage[:].rearrange("p t m j -> p m j t"),
-                in_=w_raw[b, g][:].rearrange("p j (m t) -> p m j t", t=PACK),
+                in_=w_raw[b, n][:].rearrange("p j (m t) -> p m j t", t=PACK),
             )
             flat = stage[:].rearrange("p t m j -> p (t m j)")
-            nc.vector.quantize_mx(out=w_words[b, g][:].bitcast(FP8X4), scales=w_bytes[b, g][:], in_=flat[:, 0 : 2 * W_COLS])
-            cols = slice(64 * b, 64 * (b + 1))
+            nc.vector.quantize_mx(out=w_words[b, n][:].bitcast(FP8X4), scales=w_bytes[b, n][:], in_=flat[:, 0 : 2 * W_HALF])
+            cols = slice(GROUPS * b, GROUPS * (b + 1))
             for t in (2, 3):
                 nc.vector.quantize_mx(
-                    out=w_words[t, g][:, cols].bitcast(FP8X4),
-                    scales=w_bytes[t, g][:, cols],
-                    in_=flat[:, t * W_COLS : (t + 1) * W_COLS],
+                    out=w_words[t, n][:, cols].bitcast(FP8X4),
+                    scales=w_bytes[t, n][:, cols],
+                    in_=flat[:, t * W_HALF : (t + 1) * W_HALF],
                 )
+
+        quantise_w(0, 0, nc.scalar.copy)
+        quantise_w(0, 1, nc.scalar.copy)
+        pick_words(1, 0, "w_stage0_0", S_STEPS[:1])
+        pick_words(1, 1, "w_stage0_1", S_STEPS[1:])
+        quantise_w(1, 0, nc.scalar.copy)
+        quantise_w(1, 1, nc.vector.tensor_copy)
 
         h = [keep.tile([P, S], F32, name="h%d" % c) for c in range(PACK)]
 
-        def first(c, cuts):
-            for s0, sw in cuts:
-                acc = bank("acc")
-                half, o0 = divmod(s0, BANK)
-                for g in range(PASSES):
-                    nc.tensor.matmul_mx(
-                        out=acc[:, 0:sw],
-                        lhsT=w_words[c, g][:].bitcast(FP8X4),
-                        lhsT_scale=w_bytes[c, g][:],
-                        rhs=picked_words[g, half][:, o0 : o0 + sw].bitcast(FP8X4),
-                        rhs_scale=picked_bytes[4 * g : P, s0 : s0 + sw],
-                        start=(g == 0),
-                        stop=(g == PASSES - 1),
-                    )
-                nc.scalar.activation(h[c][:, s0 : s0 + sw], acc[:, 0:sw], ACT.Gelu_apprx_tanh)
+        def first_product(c, s0, count, number):
+            acc = bank("acc_h", number)
+            half, o0 = divmod(s0, BANK)
+            for n in range(PASSES):
+                nc.tensor.matmul_mx(
+                    out=acc[:, 0:count],
+                    lhsT=w_words[c, n][:].bitcast(FP8X4),
+                    lhsT_scale=w_bytes[c, n][:],
+                    rhs=picked_words[n, half][:, o0 : o0 + count].bitcast(FP8X4),
+                    rhs_scale=picked_bytes[SCALE_ROWS * n : P, s0 : s0 + count],
+                    start=(n == 0),
+                    stop=(n == PASSES - 1),
+                )
+            nc.scalar.activation(h[c][:, s0 : s0 + count], acc[:, 0:count], ACT.Gelu_apprx_tanh)
 
-        quantise_w(0, 0, "w_stage00", nc.scalar.copy)
-        quantise_w(0, 1, "w_stage01", nc.scalar.copy)
-        pick_words(1, 0, "w_stage00", [(0, BANK)])
-        pick_words(1, 1, "w_stage01", [(0, 256), (256, 256)])
-        quantise_w(1, 0, "w_stage10", nc.scalar.copy)
-        quantise_w(1, 1, "w_stage11", nc.vector.tensor_copy)
-        first(0, S_PIECES)
-        for c in (1, 2, 3):
-            first(c, [(0, BANK), (BANK, BANK)])
+        steps = [(0, s0, count) for s0, count in S_STEPS]
+        steps = steps + [(1, s0, BANK) for s0 in range(0, S, BANK)]
+        steps = steps + [(c, s0, BANK) for s0 in range(0, S, BANK) for c in (2, 3)]
+        for number, (c, s0, count) in enumerate(steps):
+            first_product(c, s0, count, number)
 
-        g_sb = [keep.tile([P, V], F32, name="g%d" % m) for m in range(N // P)]
+        v_last, w_last = Z_PIECES[LAST]
         z_bf = [keep.tile([P, w, PACK], BF16, name="z_bf%d" % n, align_bytes=64) for n, (v0, w) in enumerate(Z_PIECES)]
-        z_q = {}
 
-        def fetch_terms(c, v0, w, terms, e):
-            for d in range(2):
+        def new_terms(name, rows, w, slot):
+            return [keep.tile([P, rows, w], F32, name="%s_%d" % (name, d), tag="terms%d_%d" % (slot, d)) for d in range(HOPS)]
+
+        def fetch_terms(c, v0, w, terms, row):
+            for d in range(HOPS):
                 nc.vector.tensor_tensor(
-                    terms[d][:, e, :],
-                    h[c][:].indirect(pos_sb[d][:, v0 // 16 : (v0 + w) // 16]),
+                    terms[d][:, row, :],
+                    h[c][:].indirect(entries(pos_sb[d], v0, w)),
                     gate_sb[:, d, v0 : v0 + w],
                     ALU.mult,
                 )
 
-        def new_terms(name, rows, w):
-            return [keep.tile([P, rows, w], F32, name="%s_%d" % (name, d)) for d in range(2)]
-
-        def turn_and_add(dst, terms, e, blk):
-            for d in range(2):
+        def turn_and_add(dst, terms, row, blk):
+            for d in range(HOPS):
                 nc.tensor.matmul(
-                    dst, terms[d][:, e, blk * P : (blk + 1) * P], ident[:], start=(d == 0), stop=(d == 1), is_transpose=True
+                    dst,
+                    terms[d][:, row, blk * P : (blk + 1) * P],
+                    ident[:],
+                    start=(d == 0),
+                    stop=(d == HOPS - 1),
+                    is_transpose=True,
                 )
 
-        low = keep.tile([P, V // P, 2, 64, 2], BF16, name="low")
+        low = [
+            keep.tile([P, v_last // P, 2, GROUPS, 2], BF16, name="low_first"),
+            keep.tile([P, w_last // P, 2, GROUPS, 2], BF16, name="low_last"),
+        ]
         for b in range(2):
-            terms = new_terms("low_terms%d" % b, 1, V)
+            terms = new_terms("low_terms%d" % b, 1, V, b)
             fetch_terms(b, 0, V, terms, 0)
-            summed = bank("summed")
+            summed = bank("summed_low", 1 + b)
             for blk in range(V // P):
                 turn_and_add(summed[:, blk * P : (blk + 1) * P], terms, 0, blk)
-            nc.scalar.copy(out=low[:, :, b, :, :], in_=summed[:].rearrange("p (k e m) -> p k m e", e=2, m=64))
-        low_words = low[:].rearrange("p k b m e -> p (k b m e)").bitcast(F32)
-        back = [bank("back%d" % n) for n in range(len(Z_PIECES))]
+            for part, (v0, v1) in enumerate([(0, v_last), (v_last, V)]):
+                nc.scalar.copy(
+                    out=low[part][:, :, b, :, :],
+                    in_=summed[:, v0:v1].rearrange("p (k e m) -> p k m e", e=2, m=GROUPS),
+                )
+
+        back = [bank("back%d" % n, 3 + n) for n in range(len(Z_PIECES))]
         for n, (v0, w) in enumerate(Z_PIECES):
+            part = 1 if n == LAST else 0
+            pairs = low[part][:].rearrange("p k b m e -> p (k b m e)").bitcast(F32)
             for blk in range(w // P):
-                k = v0 // P + blk
-                nc.tensor.transpose(back[n][:, blk * P : (blk + 1) * P], low_words[:, k * P : (k + 1) * P], ident[:])
-        last = len(Z_PIECES) - 1
-        v_last, w_last = Z_PIECES[last]
-        nc.scalar.copy(
-            out=z_bf[last][:].rearrange("p v t -> p (v t)").bitcast(F32).rearrange("p (v u) -> p v u", u=2)[:, :, 0],
-            in_=back[last][:, 0:w_last],
-        )
+                k = (v0 - part * v_last) // P + blk
+                nc.tensor.transpose(back[n][:, blk * P : (blk + 1) * P], pairs[:, k * P : (k + 1) * P], ident[:])
+        nc.scalar.copy(out=as_pairs(z_bf[LAST])[:, :, 0], in_=back[LAST][:, 0:w_last])
 
         high = {}
 
-        def sum_high(n, between=None):
+        def turn_back(n):
+            w = Z_PIECES[n][1]
+            pairs = high[n][:].rearrange("p k m e -> p (k m e)").bitcast(F32)
+            for blk in range(w // P):
+                nc.tensor.transpose(
+                    back[n][:, w + blk * P : w + (blk + 1) * P], pairs[:, blk * P : (blk + 1) * P], ident[:]
+                )
+            nc.scalar.copy(out=as_pairs(z_bf[n]), in_=back[n][:, 0 : 2 * w].rearrange("p (u v) -> p v u", u=2))
+
+        for n in range(LAST):
             v0, w = Z_PIECES[n]
-            terms = new_terms("high_terms%d" % n, 2, w)
-            summed = bank("summed")
+            terms = new_terms("high_terms%d" % n, 2, w, n % 2)
+            summed = bank("summed_high", BANKS - 1 + 2 * n)
             for e in range(2):
                 fetch_terms(2 + e, v0, w, terms, e)
                 for blk in range(w // P):
-                    turn_and_add(summed[:, (e * (w // P) + blk) * P : (e * (w // P) + blk + 1) * P], terms, e, blk)
-                if e == 0 and between is not None:
-                    turn_back(between)
+                    col = e * w + blk * P
+                    turn_and_add(summed[:, col : col + P], terms, e, blk)
+                if e == 0 and n > 0:
+                    turn_back(n - 1)
             high[n] = keep.tile([P, w // P, P, 2], BF16, name="high%d" % n)
             nc.scalar.copy(out=high[n][:], in_=summed[:, 0 : 2 * w].rearrange("p (e k m) -> p k m e", e=2, m=P))
+        turn_back(LAST - 1)
 
-        def turn_back(n):
-            v0, w = Z_PIECES[n]
-            words = high[n][:].rearrange("p k m e -> p (k m e)").bitcast(F32)
-            for blk in range(w // P):
-                nc.tensor.transpose(
-                    back[n][:, w + blk * P : w + (blk + 1) * P], words[:, blk * P : (blk + 1) * P], ident[:]
-                )
-            nc.scalar.copy(
-                out=z_bf[n][:].rearrange("p v t -> p (v t)").bitcast(F32).rearrange("p (v u) -> p v u", u=2),
-                in_=back[n][:, 0 : 2 * w].rearrange("p (u v) -> p v u", u=2),
-            )
-
-        def quantise_z(n):
-            v0, w = Z_PIECES[n]
-            z_words = keep.tile([P, w], U32, name="z_words%d" % n, align_bytes=64)
-            z_bytes = keep.tile([P, w], U8, name="z_bytes%d" % n, align_bytes=64)
-            nc.vector.quantize_mx(
-                out=z_words[:].bitcast(FP8X4), scales=z_bytes[:], in_=z_bf[n][:].rearrange("p v t -> p (v t)")
-            )
-            z_q[n] = (z_words, z_bytes)
-
-        def second(n, m):
-            v0, w = Z_PIECES[n]
-            acc2 = bank("acc2")
-            nc.tensor.matmul_mx(
-                out=acc2[:, 0:w],
-                lhsT=w2_codes[:, 2 * P * m : 2 * P * (m + 1)].bitcast(FP4X4),
-                lhsT_scale=w2_bytes[:, P * m : P * (m + 1)],
-                rhs=z_q[n][0][:].bitcast(FP8X4),
-                rhs_scale=z_q[n][1][:],
-                start=True,
-                stop=True,
-            )
-            nc.scalar.activation(g_sb[m][:, v0 : v0 + w], acc2[:, 0:w], ACT.Relu)
-
-        sum_high(0)
-        sum_high(1, between=0)
-        turn_back(1)
-        terms = new_terms("high_terms_last", 2, w_last)
+        terms = new_terms("high_terms_last", 2, w_last, LAST % 2)
         for e in range(2):
             fetch_terms(2 + e, v_last, w_last, terms, e)
         nc.vector.tensor_tensor(
-            z_bf[last][:, :, 2:4],
+            z_bf[LAST][:, :, 2:4],
             terms[0][:].rearrange("p e v -> p v e"),
             terms[1][:].rearrange("p e v -> p v e"),
             ALU.add,
         )
-        for n in (0, 2, 1):
-            quantise_z(n)
-        for m in range(N // P):
-            for n in (0, 2, 1):
-                second(n, m)
 
-        roots = {}
+        z_words = []
+        z_bytes = []
+        for n, (v0, w) in enumerate(Z_PIECES):
+            z_words.append(keep.tile([P, w], U32, name="z_words%d" % n, align_bytes=64))
+            z_bytes.append(keep.tile([P, w], U8, name="z_bytes%d" % n, align_bytes=64))
+            nc.vector.quantize_mx(
+                out=z_words[n][:].bitcast(FP8X4), scales=z_bytes[n][:], in_=z_bf[n][:].rearrange("p v t -> p (v t)")
+            )
 
-        def fetch(m, d, r0, w):
-            if (m, d) not in roots:
-                roots[m, d] = keep.tile([P, U], F32, name="root%d_%d" % (m, d))
+        g_sb = [keep.tile([P, V], F32, name="g%d" % m) for m in range(N // P)]
+
+        def second_product(m, pieces, number):
+            acc = bank("acc_g", number)
+            first = Z_PIECES[pieces[0]][0]
+            for n in pieces:
+                v0, w = Z_PIECES[n]
+                nc.tensor.matmul_mx(
+                    out=acc[:, v0 - first : v0 - first + w],
+                    lhsT=w2_codes[:, 2 * P * m : 2 * P * (m + 1)].bitcast(FP4X4),
+                    lhsT_scale=w2_bytes[:, P * m : P * (m + 1)],
+                    rhs=z_words[n][:].bitcast(FP8X4),
+                    rhs_scale=z_bytes[n][:],
+                    start=True,
+                    stop=True,
+                )
+            return g_sb[m][:, first : v0 + w], acc[:, 0 : v0 + w - first]
+
+        nc.scalar.activation(*second_product(0, [0], 4), ACT.Relu)
+        nc.vector.tensor_scalar_max(*second_product(0, [1, 2], 2), 0.0)
+        nc.scalar.activation(*second_product(1, [0, 1, 2], 4), ACT.Relu)
+
+        roots = [[keep.tile([P, U], F32, name="root%d_%d" % (m, d)) for d in range(HOPS)] for m in range(N // P)]
+        res = [keep.tile([P, U], F32, name="res%d" % m) for m in range(N // P)]
+
+        def fetch_roots(m, d, r0, w):
             nc.vector.tensor_tensor(
-                roots[m, d][:, r0 : r0 + w],
-                g_sb[m][:].indirect(nxt_sb[d][:, r0 // 16 : (r0 + w) // 16]),
+                roots[m][d][:, r0 : r0 + w],
+                g_sb[m][:].indirect(entries(nxt_sb[d], r0, w)),
                 gate2_sb[:, d, r0 : r0 + w],
                 ALU.mult,
             )
 
-        res = [keep.tile([P, U], F32, name="res%d" % m) for m in range(N // P)]
-
-        def add(m, r0, w):
+        def add_and_store(m, r0, w, queue):
             cols = slice(r0, r0 + w)
-            nc.vector.tensor_tensor(res[m][:, cols], roots[m, 0][:, cols], roots[m, 1][:, cols], ALU.add)
+            nc.vector.tensor_tensor(res[m][:, cols], roots[m][0][:, cols], roots[m][1][:, cols], ALU.add)
+            queue.dma_start(out=out[m * P : (m + 1) * P, cols], in_=res[m][:, cols])
 
-        fetch(0, 0, 0, U)
-        fetch(0, 1, 0, U)
-        fetch(1, 0, 0, U)
-        add(0, 0, U)
-        nc.sync.dma_start(out=out[0:P, :], in_=res[0][:])
-        fetch(1, 1, 0, U // 2)
-        fetch(1, 1, U // 2, U // 2)
-        add(1, 0, U // 2)
-        add(1, U // 2, U // 2)
-        nc.sync.dma_start(out=out[P : 2 * P, :], in_=res[1][:])
+        fetch_roots(0, 0, 0, U)
+        fetch_roots(0, 1, 0, U)
+        fetch_roots(1, 0, 0, U)
+        add_and_store(0, 0, U, nc.sync)
+        fetch_roots(1, 1, 0, U // 2)
+        fetch_roots(1, 1, U // 2, U // 2)
+        add_and_store(1, 0, U // 2, nc.sync)
+        add_and_store(1, U // 2, U // 2, nc.scalar)

@@ -34,7 +34,7 @@ W_HALF = H // 2
 GROUPS = W_HALF // PACK
 S_STEPS = [(0, 512), (512, 256), (768, 256)]
 Z_PIECES = [(0, 256), (256, 128), (384, 128)]
-LAST = len(Z_PIECES) - 1
+V_HALF = V // 2
 
 
 def entries(offsets, first, count):
@@ -197,20 +197,18 @@ def tile_picked_hop2_gelu_e_kernel(
         for number, (c, s0, count) in enumerate(steps):
             first_product(c, s0, count, number)
 
-        v_last, w_last = Z_PIECES[LAST]
-        z_bf = [keep.tile([P, w, PACK], BF16, name="z_bf%d" % n, align_bytes=64) for n, (v0, w) in enumerate(Z_PIECES)]
+        z_bf = [
+            keep.tile([P, w, PACK], BF16, name="z_bf%d" % n, tag="z_stage%d" % n, align_bytes=64)
+            for n, (v0, w) in enumerate(Z_PIECES)
+        ]
 
         def new_terms(name, rows, w, slot):
-            return [keep.tile([P, rows, w], F32, name="%s_%d" % (name, d), tag="terms%d_%d" % (slot, d)) for d in range(HOPS)]
+            return [
+                keep.tile([P, rows, w], F32, name="%s_%d" % (name, d), tag="terms%d_%d" % (slot, d)) for d in range(HOPS)
+            ]
 
-        def fetch_terms(c, v0, w, terms, row):
-            for d in range(HOPS):
-                nc.vector.tensor_tensor(
-                    terms[d][:, row, :],
-                    h[c][:].indirect(entries(pos_sb[d], v0, w)),
-                    gate_sb[:, d, v0 : v0 + w],
-                    ALU.mult,
-                )
+        def fetch_term(c, d, v0, w, dst):
+            nc.vector.tensor_tensor(dst, h[c][:].indirect(entries(pos_sb[d], v0, w)), gate_sb[:, d, v0 : v0 + w], ALU.mult)
 
         def turn_and_add(dst, terms, row, blk):
             for d in range(HOPS):
@@ -223,75 +221,76 @@ def tile_picked_hop2_gelu_e_kernel(
                     is_transpose=True,
                 )
 
-        low = [
-            keep.tile([P, v_last // P, 2, GROUPS, 2], BF16, name="low_first"),
-            keep.tile([P, w_last // P, 2, GROUPS, 2], BF16, name="low_last"),
-        ]
+        low = keep.tile([P, V // P, 2, GROUPS, 2], BF16, name="low")
         for b in range(2):
             terms = new_terms("low_terms%d" % b, 1, V, b)
-            fetch_terms(b, 0, V, terms, 0)
+            for d in range(HOPS):
+                fetch_term(b, d, 0, V, terms[d][:, 0, :])
             summed = bank("summed_low", 1 + b)
             for blk in range(V // P):
                 turn_and_add(summed[:, blk * P : (blk + 1) * P], terms, 0, blk)
-            for part, (v0, v1) in enumerate([(0, v_last), (v_last, V)]):
-                nc.scalar.copy(
-                    out=low[part][:, :, b, :, :],
-                    in_=summed[:, v0:v1].rearrange("p (k e m) -> p k m e", e=2, m=GROUPS),
-                )
+            nc.scalar.copy(out=low[:, :, b, :, :], in_=summed[:].rearrange("p (k e m) -> p k m e", e=2, m=GROUPS))
 
-        back = [bank("back%d" % n, 3 + n) for n in range(len(Z_PIECES))]
-        for n, (v0, w) in enumerate(Z_PIECES):
-            part = 1 if n == LAST else 0
-            pairs = low[part][:].rearrange("p k b m e -> p (k b m e)").bitcast(F32)
-            for blk in range(w // P):
-                k = (v0 - part * v_last) // P + blk
-                nc.tensor.transpose(back[n][:, blk * P : (blk + 1) * P], pairs[:, k * P : (k + 1) * P], ident[:])
-        nc.scalar.copy(out=as_pairs(z_bf[LAST])[:, :, 0], in_=back[LAST][:, 0:w_last])
-
-        high = {}
-
-        def turn_back(n):
-            w = Z_PIECES[n][1]
-            pairs = high[n][:].rearrange("p k m e -> p (k m e)").bitcast(F32)
-            for blk in range(w // P):
-                nc.tensor.transpose(
-                    back[n][:, w + blk * P : w + (blk + 1) * P], pairs[:, blk * P : (blk + 1) * P], ident[:]
-                )
-            nc.scalar.copy(out=as_pairs(z_bf[n]), in_=back[n][:, 0 : 2 * w].rearrange("p (u v) -> p v u", u=2))
-
-        for n in range(LAST):
+        low_pairs = low[:].rearrange("p k b m e -> p (k b m e)").bitcast(F32)
+        back_first = bank("back_first", 3)
+        back_rest = bank("back_rest", 4)
+        for blk in range(V // P):
+            dst = back_first if blk * P < V_HALF else back_rest
+            col = blk * P % V_HALF
+            nc.tensor.transpose(dst[:, col : col + P], low_pairs[:, blk * P : (blk + 1) * P], ident[:])
+        for n in (1, 2):
             v0, w = Z_PIECES[n]
-            terms = new_terms("high_terms%d" % n, 2, w, n % 2)
-            summed = bank("summed_high", BANKS - 1 + 2 * n)
-            for e in range(2):
-                fetch_terms(2 + e, v0, w, terms, e)
-                for blk in range(w // P):
-                    col = e * w + blk * P
-                    turn_and_add(summed[:, col : col + P], terms, e, blk)
-                if e == 0 and n > 0:
-                    turn_back(n - 1)
-            high[n] = keep.tile([P, w // P, P, 2], BF16, name="high%d" % n)
-            nc.scalar.copy(out=high[n][:], in_=summed[:, 0 : 2 * w].rearrange("p (e k m) -> p k m e", e=2, m=P))
-        turn_back(LAST - 1)
+            nc.scalar.copy(out=as_pairs(z_bf[n])[:, :, 0], in_=back_rest[:, v0 - V_HALF : v0 - V_HALF + w])
 
-        terms = new_terms("high_terms_last", 2, w_last, LAST % 2)
+        terms = new_terms("high_terms_first", 2, V_HALF, 0)
+        summed = bank("summed_high", 7)
         for e in range(2):
-            fetch_terms(2 + e, v_last, w_last, terms, e)
-        nc.vector.tensor_tensor(
-            z_bf[LAST][:, :, 2:4],
-            terms[0][:].rearrange("p e v -> p v e"),
-            terms[1][:].rearrange("p e v -> p v e"),
-            ALU.add,
-        )
+            for d in range(HOPS):
+                fetch_term(2 + e, d, 0, V_HALF, terms[d][:, e, :])
+            for blk in range(V_HALF // P):
+                col = e * V_HALF + blk * P
+                turn_and_add(summed[:, col : col + P], terms, e, blk)
+        high = keep.tile([P, V_HALF // P, P, 2], BF16, name="high")
+        nc.scalar.copy(out=high[:], in_=summed[:].rearrange("p (e k m) -> p k m e", e=2, m=P))
+        high_pairs = high[:].rearrange("p k m e -> p (k m e)").bitcast(F32)
+        for blk in range(V_HALF // P):
+            col = V_HALF + blk * P
+            nc.tensor.transpose(back_first[:, col : col + P], high_pairs[:, blk * P : (blk + 1) * P], ident[:])
+        nc.scalar.copy(out=as_pairs(z_bf[0]), in_=back_first[:].rearrange("p (u v) -> p v u", u=2))
 
-        z_words = []
-        z_bytes = []
-        for n, (v0, w) in enumerate(Z_PIECES):
-            z_words.append(keep.tile([P, w], U32, name="z_words%d" % n, align_bytes=64))
-            z_bytes.append(keep.tile([P, w], U8, name="z_bytes%d" % n, align_bytes=64))
+        z_words = {}
+        z_bytes = {}
+
+        def quantise_z(n, tag):
+            w = Z_PIECES[n][1]
+            z_words[n] = keep.tile([P, w], U32, name="z_words%d" % n, tag=tag, align_bytes=64)
+            z_bytes[n] = keep.tile([P, w], U8, name="z_bytes%d" % n, align_bytes=64)
             nc.vector.quantize_mx(
                 out=z_words[n][:].bitcast(FP8X4), scales=z_bytes[n][:], in_=z_bf[n][:].rearrange("p v t -> p (v t)")
             )
+
+        terms = new_terms("high_terms_rest", 2, V_HALF, 1)
+
+        def fetch_upper(n, d):
+            v0, w = Z_PIECES[n]
+            fetch_term(3, d, v0, w, terms[d][:, 1, v0 - V_HALF : v0 - V_HALF + w])
+
+        def add_upper(n):
+            v0, w = Z_PIECES[n]
+            both = [terms[d][:, :, v0 - V_HALF : v0 - V_HALF + w].rearrange("p e v -> p v e") for d in range(HOPS)]
+            nc.vector.tensor_tensor(z_bf[n][:, :, 2:4], both[0], both[1], ALU.add)
+
+        for d in range(HOPS):
+            fetch_term(2, d, V_HALF, V_HALF, terms[d][:, 0, :])
+        fetch_upper(1, 0)
+        fetch_upper(1, 1)
+        fetch_upper(2, 0)
+        add_upper(1)
+        fetch_upper(2, 1)
+        quantise_z(1, "z_words1")
+        add_upper(2)
+        quantise_z(0, "z_words0")
+        quantise_z(2, "z_stage0")
 
         g_sb = [keep.tile([P, V], F32, name="g%d" % m) for m in range(N // P)]
 
@@ -309,11 +308,12 @@ def tile_picked_hop2_gelu_e_kernel(
                     start=True,
                     stop=True,
                 )
-            return g_sb[m][:, first : v0 + w], acc[:, 0 : v0 + w - first]
+            nc.scalar.activation(g_sb[m][:, first : v0 + w], acc[:, 0 : v0 + w - first], ACT.Relu)
 
-        nc.scalar.activation(*second_product(0, [0], 4), ACT.Relu)
-        nc.vector.tensor_scalar_max(*second_product(0, [1, 2], 2), 0.0)
-        nc.scalar.activation(*second_product(1, [0, 1, 2], 4), ACT.Relu)
+        second_product(0, [1], 3)
+        second_product(0, [0], 5)
+        second_product(0, [2], 6)
+        second_product(1, [0, 1, 2], 1)
 
         roots = [[keep.tile([P, U], F32, name="root%d_%d" % (m, d)) for d in range(HOPS)] for m in range(N // P)]
         res = [keep.tile([P, U], F32, name="res%d" % m) for m in range(N // P)]
@@ -326,16 +326,17 @@ def tile_picked_hop2_gelu_e_kernel(
                 ALU.mult,
             )
 
-        def add_and_store(m, r0, w, queue):
+        def add_roots(m, r0, w):
             cols = slice(r0, r0 + w)
             nc.vector.tensor_tensor(res[m][:, cols], roots[m][0][:, cols], roots[m][1][:, cols], ALU.add)
-            queue.dma_start(out=out[m * P : (m + 1) * P, cols], in_=res[m][:, cols])
 
         fetch_roots(0, 0, 0, U)
         fetch_roots(0, 1, 0, U)
         fetch_roots(1, 0, 0, U)
-        add_and_store(0, 0, U, nc.sync)
+        add_roots(0, 0, U)
+        nc.sync.dma_start(out=out[0:P, :], in_=res[0][:])
         fetch_roots(1, 1, 0, U // 2)
         fetch_roots(1, 1, U // 2, U // 2)
-        add_and_store(1, 0, U // 2, nc.sync)
-        add_and_store(1, U // 2, U // 2, nc.scalar)
+        add_roots(1, 0, U // 2)
+        add_roots(1, U // 2, U // 2)
+        nc.sync.dma_start(out=out[P : 2 * P, :], in_=res[1][:])

@@ -63,11 +63,6 @@ def tile_picked_hop2_gelu_e_kernel(
         def bank(name, number):
             return psum.tile([P, BANK], F32, name=name, tag="bank%d" % (number % BANKS))
 
-        warm_in = keep.tile([P, 8], F32, name="warm_in")
-        warm_out = keep.tile([P, 8], F32, name="warm_out")
-        nc.vector.memset(warm_in[:], 0.0)
-        nc.scalar.activation(warm_out[:], warm_in[:], ACT.Gelu_apprx_tanh)
-
         x_bytes = keep.tile([P, T], U8, name="x_bytes", align_bytes=64)
         nc.gpsimd.memset(x_bytes[:], 0)
         w2_bytes = keep.tile([P, N], U8, name="w2_bytes", align_bytes=64)

from contextlib import ExitStack

import concourse.mybir as mybir
from concourse.masks import make_identity

K, T, S, V, H, N, U = 1024, 2048, 1024, 512, 512, 256, 256
FLOPS = 2 * K * H * S + 2 * H * N * V

F32 = mybir.dt.float32
BF16 = mybir.dt.bfloat16
I32 = mybir.dt.int32
U32 = mybir.dt.uint32
U16 = mybir.dt.uint16
U8 = mybir.dt.uint8
FP8X4 = mybir.dt.float8_e4m3fn_x4
FP4X4 = mybir.dt.float4_e2m1fn_x4
ACT = mybir.ActivationFunctionType
ALU = mybir.AluOpType

P = 128
PACK = 4
K_PASS = P * PACK
PASSES = K // K_PASS
BANK = 512
BANKS = 8
PER_COLUMN = 16
SCALE_ROWS = 4
HOPS = 2

X_LOADS = [[1280, 768], [1024, 512, 256, 256]]
X_ON_VECTOR = [[640, 384], [512, 192, 96, 128]]
X_QUANT = 512
W_HALF = H // 2
GROUPS = W_HALF // PACK
S_STEPS = [(0, 512), (512, 256), (768, 256)]
Z_PIECES = [(0, 256), (256, 128), (384, 128)]
V_HALF = V // 2


def entries(offsets, first, count):
    return offsets[:, first // PER_COLUMN : (first + count) // PER_COLUMN]


def interleave(copy, grouped, raw, c0, c1):
    copy(
        out=grouped[:, c0:c1, :].rearrange("p (c i) t -> p c t i", i=4),
        in_=raw[:, :, c0:c1].rearrange("p t (c i) -> p c t i", i=4),
    )


def as_pairs(tile):
    return tile[:].rearrange("p v t -> p (v t)").bitcast(F32).rearrange("p (v u) -> p v u", u=2)


def tile_picked_hop2_gelu_e_kernel(
    tc, xT, w1, w2_words, w2_scales, gate, gate2, offs, pos1, pos2, nxt1, nxt2, out
):
    nc = tc.nc
    with ExitStack() as ctx:
        keep = ctx.enter_context(tc.tile_pool(name="keep", bufs=1))
        psum = ctx.enter_context(tc.psum_pool(name="psum", bufs=1))

        def bank(name, number):
            return psum.tile([P, BANK], F32, name=name, tag="bank%d" % (number % BANKS))

        x_bytes = keep.tile([P, T], U8, name="x_bytes", align_bytes=64)
        nc.gpsimd.memset(x_bytes[:], 0)
        w2_bytes = keep.tile([P, N], U8, name="w2_bytes", align_bytes=64)
        nc.gpsimd.memset(w2_bytes[:], 0)
        ident = keep.tile([P, P], F32, name="ident")
        make_identity(nc, ident[:])

        offs_sb = keep.tile([P, S // PER_COLUMN], U16, name="offs_sb")
        pos_sb = [keep.tile([P, V // PER_COLUMN], U16, name="pos%d" % d) for d in range(HOPS)]
        nxt_sb = [keep.tile([P, U // PER_COLUMN], U16, name="nxt%d" % d) for d in range(HOPS)]
        x_raw = {}
        for n in range(PASSES):
            rows = xT[n * K_PASS : (n + 1) * K_PASS, :].rearrange("(p j) w -> p j w", j=PACK)
            c0 = 0
            for load, width in enumerate(X_LOADS[n]):
                x_raw[n, load] = keep.tile([P, PACK, width], F32, name="x_raw%d_%d" % (n, load))
                nc.sync.dma_start(out=x_raw[n, load][:], in_=rows[:, :, c0 : c0 + width])
                c0 = c0 + width
                if (n, load) == (0, 0):
                    nc.sync.dma_start(offs_sb[:], offs)
                    nc.sync.dma_start(pos_sb[0][:], pos1)
                    nc.sync.dma_start(pos_sb[1][:], pos2)
        w_raw = {}
        for b in range(H // W_HALF):
            for n in range(PASSES):
                rows = w1[n * K_PASS : (n + 1) * K_PASS, :].rearrange("(p j) w -> p j w", j=PACK)
                w_raw[b, n] = keep.tile([P, PACK, W_HALF], F32, name="w_raw%d_%d" % (b, n))
                nc.sync.dma_start(out=w_raw[b, n][:], in_=rows[:, :, b * W_HALF : (b + 1) * W_HALF])
        gate_sb = keep.tile([P, HOPS, V], F32, name="gate_sb")
        for d in range(HOPS):
            nc.sync.dma_start(out=gate_sb[:, d, :], in_=gate[d])
        gate2_sb = keep.tile([P, HOPS, U], F32, name="gate2_sb")
        nc.sync.dma_start(out=gate2_sb[:], in_=gate2.rearrange("d p v -> p d v"))
        nc.sync.dma_start(nxt_sb[0][:], nxt1)
        nc.sync.dma_start(nxt_sb[1][:], nxt2)
        w2_codes = keep.tile([P, 2 * N], U8, name="w2_codes", align_bytes=64)
        nc.sync.dma_start(out=w2_codes[:].bitcast(I32), in_=w2_words[0].bitcast(I32))
        for q in range(P // 32):
            nc.sync.dma_start(
                out=w2_bytes[32 * q : 32 * q + SCALE_ROWS, :].bitcast(I32),
                in_=w2_scales[0, SCALE_ROWS * q : SCALE_ROWS * (q + 1), :].bitcast(I32),
            )

        x_words = [keep.tile([P, T], U32, name="x_words%d" % n, align_bytes=64) for n in range(PASSES)]
        picked_words = {}

        def pick_words(n, half, tag, steps):
            picked = keep.tile([P, BANK], U32, name="picked%d_%d" % (n, half), tag=tag, align_bytes=64)
            for s0, count in steps:
                o0 = s0 - half * BANK
                nc.vector.tensor_copy(picked[:, o0 : o0 + count], x_words[n][:].indirect(entries(offs_sb, s0, count)))
            picked_words[n, half] = picked

        for n in range(PASSES):
            c0 = 0
            for load, width in enumerate(X_LOADS[n]):
                grouped = keep.tile([P, width, PACK], BF16, name="x_bf%d_%d" % (n, load), align_bytes=64)
                split = X_ON_VECTOR[n][load]
                interleave(nc.vector.tensor_copy, grouped, x_raw[n, load], 0, split)
                interleave(nc.scalar.copy, grouped, x_raw[n, load], split, width)
                for q1 in range(width % X_QUANT or X_QUANT, width + 1, X_QUANT):
                    q0 = max(0, q1 - X_QUANT)
                    nc.vector.quantize_mx(
                        out=x_words[n][:, c0 + q0 : c0 + q1].bitcast(FP8X4),
                        scales=x_bytes[SCALE_ROWS * n : P, c0 + q0 : c0 + q1],
                        in_=grouped[:, q0:q1, :].rearrange("p w j -> p (w j)"),
                    )
                c0 = c0 + width
            if n == 0:
                for half in range(S // BANK):
                    pick_words(0, half, "picked_first%d" % half, [(half * BANK, BANK)])
        picked_bytes = keep.tile([P, S], U8, name="picked_bytes", align_bytes=64)
        nc.vector.tensor_copy(picked_bytes[:], x_bytes[:].indirect(offs_sb[:]))

        w_words = {}
        w_bytes = {}
        for c in range(PACK):
            for n in range(PASSES):
                w_words[c, n] = keep.tile([P, P], U32, name="w_words%d_%d" % (c, n), align_bytes=64)
                w_bytes[c, n] = keep.tile([P, P], U8, name="w_bytes%d_%d" % (c, n), align_bytes=64)

        def quantise_w(b, n, copy):
            stage = keep.tile(
                [P, PACK, GROUPS, PACK], BF16, name="w_bf%d_%d" % (b, n), tag="w_stage%d_%d" % (b, n), align_bytes=64
            )
            copy(
                out=stage[:].rearrange("p t m j -> p m j t"),
                in_=w_raw[b, n][:].rearrange("p j (m t) -> p m j t", t=PACK),
            )
            flat = stage[:].rearrange("p t m j -> p (t m j)")
            nc.vector.quantize_mx(out=w_words[b, n][:].bitcast(FP8X4), scales=w_bytes[b, n][:], in_=flat[:, 0 : 2 * W_HALF])
            cols = slice(GROUPS * b, GROUPS * (b + 1))
            for t in (2, 3):
                nc.vector.quantize_mx(
                    out=w_words[t, n][:, cols].bitcast(FP8X4),
                    scales=w_bytes[t, n][:, cols],
                    in_=flat[:, t * W_HALF : (t + 1) * W_HALF],
                )

        quantise_w(0, 0, nc.scalar.copy)
        quantise_w(0, 1, nc.scalar.copy)
        pick_words(1, 0, "w_stage0_0", S_STEPS[:1])
        pick_words(1, 1, "w_stage0_1", S_STEPS[1:])
        quantise_w(1, 0, nc.scalar.copy)
        quantise_w(1, 1, nc.vector.tensor_copy)

        h = [keep.tile([P, S], F32, name="h%d" % c) for c in range(PACK)]

        def first_product(c, s0, count, number):
            acc = bank("acc_h", number)
            half, o0 = divmod(s0, BANK)
            for n in range(PASSES):
                nc.tensor.matmul_mx(
                    out=acc[:, 0:count],
                    lhsT=w_words[c, n][:].bitcast(FP8X4),
                    lhsT_scale=w_bytes[c, n][:],
                    rhs=picked_words[n, half][:, o0 : o0 + count].bitcast(FP8X4),
                    rhs_scale=picked_bytes[SCALE_ROWS * n : P, s0 : s0 + count],
                    start=(n == 0),
                    stop=(n == PASSES - 1),
                )
            nc.scalar.activation(h[c][:, s0 : s0 + count], acc[:, 0:count], ACT.Gelu_apprx_tanh)

        steps = [(0, s0, count) for s0, count in S_STEPS]
        steps = steps + [(1, s0, BANK) for s0 in range(0, S, BANK)]
        steps = steps + [(c, s0, BANK) for s0 in range(0, S, BANK) for c in (2, 3)]
        for number, (c, s0, count) in enumerate(steps):
            first_product(c, s0, count, number)

        z_bf = [
            keep.tile([P, w, PACK], BF16, name="z_bf%d" % n, tag="z_stage%d" % n, align_bytes=64)
            for n, (v0, w) in enumerate(Z_PIECES)
        ]

        def new_terms(name, rows, w, slot):
            return [
                keep.tile([P, rows, w], F32, name="%s_%d" % (name, d), tag="terms%d_%d" % (slot, d)) for d in range(HOPS)
            ]

        def fetch_term(c, d, v0, w, dst):
            nc.vector.tensor_tensor(dst, h[c][:].indirect(entries(pos_sb[d], v0, w)), gate_sb[:, d, v0 : v0 + w], ALU.mult)

        def turn_and_add(dst, terms, row, blk):
            for d in range(HOPS):
                nc.tensor.matmul(
                    dst,
                    terms[d][:, row, blk * P : (blk + 1) * P],
                    ident[:],
                    start=(d == 0),
                    stop=(d == HOPS - 1),
                    is_transpose=True,
                )

        low = keep.tile([P, V // P, 2, GROUPS, 2], BF16, name="low")
        for b in range(2):
            terms = new_terms("low_terms%d" % b, 1, V, b)
            for d in range(HOPS):
                fetch_term(b, d, 0, V, terms[d][:, 0, :])
            summed = bank("summed_low", 1 + b)
            for blk in range(V // P):
                turn_and_add(summed[:, blk * P : (blk + 1) * P], terms, 0, blk)
            nc.scalar.copy(out=low[:, :, b, :, :], in_=summed[:].rearrange("p (k e m) -> p k m e", e=2, m=GROUPS))

        low_pairs = low[:].rearrange("p k b m e -> p (k b m e)").bitcast(F32)
        back_first = bank("back_first", 3)
        back_rest = bank("back_rest", 4)
        for blk in range(V // P):
            dst = back_first if blk * P < V_HALF else back_rest
            col = blk * P % V_HALF
            nc.tensor.transpose(dst[:, col : col + P], low_pairs[:, blk * P : (blk + 1) * P], ident[:])
        for n in (1, 2):
            v0, w = Z_PIECES[n]
            nc.scalar.copy(out=as_pairs(z_bf[n])[:, :, 0], in_=back_rest[:, v0 - V_HALF : v0 - V_HALF + w])

        terms = new_terms("high_terms_first", 2, V_HALF, 0)
        summed = bank("summed_high", 7)
        for e in range(2):
            for d in range(HOPS):
                fetch_term(2 + e, d, 0, V_HALF, terms[d][:, e, :])
            for blk in range(V_HALF // P):
                col = e * V_HALF + blk * P
                turn_and_add(summed[:, col : col + P], terms, e, blk)
        high = keep.tile([P, V_HALF // P, P, 2], BF16, name="high")
        nc.scalar.copy(out=high[:], in_=summed[:].rearrange("p (e k m) -> p k m e", e=2, m=P))
        high_pairs = high[:].rearrange("p k m e -> p (k m e)").bitcast(F32)
        for blk in range(V_HALF // P):
            col = V_HALF + blk * P
            nc.tensor.transpose(back_first[:, col : col + P], high_pairs[:, blk * P : (blk + 1) * P], ident[:])
        nc.scalar.copy(out=as_pairs(z_bf[0]), in_=back_first[:].rearrange("p (u v) -> p v u", u=2))

        z_words = {}
        z_bytes = {}

        def quantise_z(n, tag):
            w = Z_PIECES[n][1]
            z_words[n] = keep.tile([P, w], U32, name="z_words%d" % n, tag=tag, align_bytes=64)
            z_bytes[n] = keep.tile([P, w], U8, name="z_bytes%d" % n, align_bytes=64)
            nc.vector.quantize_mx(
                out=z_words[n][:].bitcast(FP8X4), scales=z_bytes[n][:], in_=z_bf[n][:].rearrange("p v t -> p (v t)")
            )

        terms = new_terms("high_terms_rest", 2, V_HALF, 1)

        def fetch_upper(n, d):
            v0, w = Z_PIECES[n]
            fetch_term(3, d, v0, w, terms[d][:, 1, v0 - V_HALF : v0 - V_HALF + w])

        def add_upper(n):
            v0, w = Z_PIECES[n]
            both = [terms[d][:, :, v0 - V_HALF : v0 - V_HALF + w].rearrange("p e v -> p v e") for d in range(HOPS)]
            nc.vector.tensor_tensor(z_bf[n][:, :, 2:4], both[0], both[1], ALU.add)

        for d in range(HOPS):
            fetch_term(2, d, V_HALF, V_HALF, terms[d][:, 0, :])
        fetch_upper(1, 0)
        fetch_upper(1, 1)
        fetch_upper(2, 0)
        add_upper(1)
        fetch_upper(2, 1)
        quantise_z(1, "z_words1")
        add_upper(2)
        quantise_z(0, "z_words0")
        quantise_z(2, "z_stage0")

        g_sb = [keep.tile([P, V], F32, name="g%d" % m) for m in range(N // P)]

        def second_product(m, pieces, number):
            acc = bank("acc_g", number)
            first = Z_PIECES[pieces[0]][0]
            for n in pieces:
                v0, w = Z_PIECES[n]
                nc.tensor.matmul_mx(
                    out=acc[:, v0 - first : v0 - first + w],
                    lhsT=w2_codes[:, 2 * P * m : 2 * P * (m + 1)].bitcast(FP4X4),
                    lhsT_scale=w2_bytes[:, P * m : P * (m + 1)],
                    rhs=z_words[n][:].bitcast(FP8X4),
                    rhs_scale=z_bytes[n][:],
                    start=True,
                    stop=True,
                )
            nc.scalar.activation(g_sb[m][:, first : v0 + w], acc[:, 0 : v0 + w - first], ACT.Relu)

        second_product(0, [1], 3)
        second_product(0, [0], 5)
        second_product(0, [2], 6)
        second_product(1, [0, 1, 2], 1)

        roots = [[keep.tile([P, U], F32, name="root%d_%d" % (m, d)) for d in range(HOPS)] for m in range(N // P)]
        res = [keep.tile([P, U], F32, name="res%d" % m) for m in range(N // P)]

        def fetch_roots(m, d, r0, w):
            nc.vector.tensor_tensor(
                roots[m][d][:, r0 : r0 + w],
                g_sb[m][:].indirect(entries(nxt_sb[d], r0, w)),
                gate2_sb[:, d, r0 : r0 + w],
                ALU.mult,
            )

        def add_roots(m, r0, w):
            cols = slice(r0, r0 + w)
            nc.vector.tensor_tensor(res[m][:, cols], roots[m][0][:, cols], roots[m][1][:, cols], ALU.add)

        fetch_roots(0, 0, 0, U)
        fetch_roots(0, 1, 0, U)
        fetch_roots(1, 0, 0, U)
        add_roots(0, 0, U)
        nc.sync.dma_start(out=out[0:P, :], in_=res[0][:])
        fetch_roots(1, 1, 0, U // 2)
        fetch_roots(1, 1, U // 2, U // 2)
        add_roots(1, 0, U // 2)
        add_roots(1, U // 2, U // 2)
        nc.sync.dma_start(out=out[P : 2 * P, :], in_=res[1][:])
